import numpy as np
import ml_dtypes


def mxq(x, axis, fmt="e4m3"):
    dtype, down = {"e4m3": (ml_dtypes.float8_e4m3fn, 7), "e5m2": (ml_dtypes.float8_e5m2, 14)}[fmt]
    v = np.moveaxis(np.asarray(x, np.float32).astype(ml_dtypes.bfloat16).astype(np.float64), axis, -1)
    blocks = v.reshape(v.shape[:-1] + (-1, 32))
    amax = np.abs(blocks).max(-1, keepdims=True)
    byte = np.maximum(np.where(amax > 0, np.frexp(amax)[1] - 1 + 127, 0) - down, 1)
    scale = np.exp2(byte - 127.0)
    codes = (blocks / scale).astype(np.float32).astype(dtype).astype(np.float64)
    return np.moveaxis((codes * scale).reshape(v.shape), -1, axis)


WIDE = False


def mx_kscale(k):
    if not WIDE:
        return np.ones(k)
    levels = np.array([10, -10, 5, -5, 0])
    if k % 512:
        return np.exp2(np.random.permutation(np.resize(levels, k // 32))).repeat(32)
    a = np.empty((k // 512, 16))
    for p in range(k // 512):
        a[p, :8] = np.random.permutation(np.resize(levels, 8))
        for g in range(8):
            far = levels[np.abs(levels - a[p, g]) >= 10]
            a[p, g + 8] = far[np.random.randint(len(far))]
    return np.exp2(a.ravel()).repeat(32)


BF16 = ml_dtypes.bfloat16


def bf(x):
    return np.asarray(x, np.float32).astype(BF16)


def f64(x):
    return np.asarray(x).astype(np.float64)


E2M1 = np.array([0.0, 0.5, 1.0, 1.5, 2.0, 3.0, 4.0, 6.0, -0.0, -0.5, -1.0, -1.5, -2.0, -3.0, -4.0, -6.0])


def pack_weight(w, fmt):
    k, n = w.shape
    w = f64(bf(w)).reshape(k // 32, 32, n)
    amax = np.abs(w).max(1)
    if fmt == "e4m3":
        byte = np.frexp(amax)[1] - 1 + 127 - 7
    else:
        mant, ex = np.frexp(amax / 6.0)
        byte = np.where(mant > 0.5, ex, ex - 1) + 127
    byte = np.clip(np.where(amax > 0, byte, 1), 1, 254)
    scaled = (w * np.exp2(127.0 - byte)[:, None, :]).reshape(k, n).astype(np.float32)
    by_word = np.ascontiguousarray(scaled.reshape(k // 512, 128, 4, n).transpose(0, 1, 3, 2))
    if fmt == "e4m3":
        words = by_word.astype(ml_dtypes.float8_e4m3fn).view(np.uint8)
    else:
        c = by_word.astype(ml_dtypes.float4_e2m1fn).view(np.uint8) & 0xF
        words = c[..., 0::2] | (c[..., 1::2] << 4)
    return np.ascontiguousarray(words), np.ascontiguousarray(byte.astype(np.uint8).reshape(k // 512, 16, n))


def unpack_weight(words, scales, fmt):
    g, p, n, _ = words.shape
    if fmt == "e4m3":
        vals = np.ascontiguousarray(words).view(ml_dtypes.float8_e4m3fn).astype(np.float64)
    else:
        nib = np.empty((g, p, n, 4), np.uint8)
        nib[..., 0::2] = words & 0xF
        nib[..., 1::2] = words >> 4
        vals = E2M1[nib]
    vals = vals * np.repeat(np.exp2(scales.astype(np.float64) - 127.0), 8, axis=1)[..., None]
    return vals.transpose(0, 1, 3, 2).reshape(g * 512, n)
def pack4(w):
    words, scales = pack_weight(w, "e2m1")
    return words.reshape(words.shape[0], 128, -1), scales


def unpack4(words, scales):
    return unpack_weight(words.reshape(words.shape[0], 128, -1, 2), scales, "e2m1")


T, K, R, C = 2048, 1024, 512, 1024


def draw0():
    s = mx_kscale(K)
    v = mx_kscale(T)
    a = T ** -0.25
    far = np.random.standard_normal((T, K)) * s * v[:, None]
    mic = np.random.standard_normal((T, C)) * v[:, None]
    path = np.random.standard_normal((K, C)) / np.sqrt(K) / s[:, None]
    basis = np.random.standard_normal((K, R)) / np.sqrt(K) * a / s[:, None]
    basis_words, basis_scales = pack4(basis)
    step = (0.5 + np.random.random(T)) * a / v ** 2
    gain = 0.5 + np.random.random(R)
    return {"far": bf(far),
            "mic": bf(mic),
            "path": bf(path),
            "basis_words": basis_words,
            "basis_scales": basis_scales,
            "step": bf(step),
            "gain": bf(gain)}


def core(far, mic, path, basis_words, basis_scales, step, gain):
    x = mxq(f64(far), 1, "e4m3")
    echo = x @ mxq(f64(path), 0, "e4m3")
    u = x @ unpack4(basis_words, basis_scales)
    e = (f64(mic) - echo) * f64(step)[:, None]
    grad = mxq(u, 0, "e4m3").T @ mxq(e, 0, "e4m3")
    return grad * f64(gain)[:, None]


def e4m3fn_bytes(y):
    return np.clip(np.asarray(y, np.float64), -448.0, 448.0).astype(np.float32).astype(ml_dtypes.float8_e4m3fn).view(np.uint8)


def e4m3fn_values(b):
    return np.asarray(b, np.uint8).view(ml_dtypes.float8_e4m3fn).astype(np.float64)


def setup_inputs():
    d = draw0()
    x0 = np.asarray(d['path']).astype(np.float64)
    s = (np.max(np.abs(x0), axis=(1,), keepdims=True) / 448.0).astype(np.float32)
    out = {}
    for k, v in d.items():
        if k == 'path':
            out['path_bytes'] = e4m3fn_bytes(x0 / s.astype(np.float64))
            out['path_scale'] = s
        else:
            out[k] = v
    return out


def reference(far, mic, path_bytes, path_scale, basis_words, basis_scales, step, gain):
    return core(far, mic, e4m3fn_values(path_bytes) * path_scale.astype(np.float64), basis_words, basis_scales, step, gain)

@@ -1,0 +1,578 @@
+from contextlib import ExitStack
+
+import concourse.mybir as mybir
+from concourse.masks import make_identity
+
+T, K, R, C = 2048, 1024, 512, 1024
+FLOPS = 2 * T * K * C + 2 * T * K * R + 2 * T * R * C
+
+F32 = mybir.dt.float32
+BF16 = mybir.dt.bfloat16
+I32 = mybir.dt.int32
+U32 = mybir.dt.uint32
+U8 = mybir.dt.uint8
+FP8 = mybir.dt.float8_e4m3fn
+FP8X4 = mybir.dt.float8_e4m3fn_x4
+FP4X4 = mybir.dt.float4_e2m1fn_x4
+ALU = mybir.AluOpType
+COPY = mybir.ActivationFunctionType.Copy
+
+P = 128
+PACK = 4
+PASS = P * PACK
+NG = T // PASS
+NK = K // PASS
+NH = 2
+W = C // NH
+
+
+def tile_echo_nlms_gradient_s11_kernel(
+    tc, far, mic, path_bytes, path_scale, basis_words, basis_scales, step, gain, out
+):
+    nc = tc.nc
+    with ExitStack() as ctx:
+        keep = ctx.enter_context(tc.tile_pool(name="keep", bufs=1))
+        work = ctx.enter_context(tc.tile_pool(name="work", bufs=2))
+        turn = ctx.enter_context(tc.psum_pool(name="turn", bufs=2))
+        comp = ctx.enter_context(tc.psum_pool(name="comp", bufs=2))
+        echo = ctx.enter_context(tc.psum_pool(name="echo", bufs=4))
+
+        pscale = keep.tile([P, NK, PACK], F32, name="pscale")
+        nc.scalar.dma_start(out=pscale[:], in_=path_scale.rearrange("(g p t) o -> p g (t o)", p=P, t=PACK))
+        step_bf = keep.tile([P, NG, PACK], BF16, name="step_bf")
+        nc.gpsimd.dma_start(out=step_bf[:], in_=step.rearrange("(g p j) -> p g j", p=P, j=PACK))
+        gain_bf = keep.tile([P, PACK], BF16, name="gain_bf")
+        nc.gpsimd.dma_start(out=gain_bf[:], in_=gain.rearrange("(q m) -> q m", m=PACK))
+
+        ident = keep.tile([P, P], F32, name="ident")
+        make_identity(nc, ident[:])
+        bscale = keep.tile([P, NK, R], U8, name="bscale", align_bytes=64)
+        nc.vector.memset(bscale[:].rearrange("p g n -> p (g n)").bitcast(I32), 0)
+
+        far_t = [keep.tile([P, PACK, K], BF16, name=f"far{g}") for g in range(NG)]
+        mic_t = [[keep.tile([P, PACK, W], BF16, name=f"mic{g}_{h}") for h in range(NH)] for g in range(NG)]
+        pbytes = [keep.tile([P, PACK, C], U8, name=f"pbytes{g}", align_bytes=64) for g in range(NK)]
+        bwords = keep.tile([P, NK, 2 * R], U8, name="bwords", align_bytes=64)
+        far_v = far.rearrange("(g p j) k -> g p j k", p=P, j=PACK)
+        mic_v = mic.rearrange("(g p j) c -> g p j c", p=P, j=PACK)
+        path_v = path_bytes.rearrange("(g p t) c -> g p t c", p=P, t=PACK)
+
+        def load_far(g, half):
+            js = slice(2 * half, 2 * half + 2)
+            nc.sync.dma_start(out=far_t[g][:, js, :], in_=far_v[g][:, js, :])
+
+        def load_mic(g, h):
+            nc.sync.dma_start(out=mic_t[g][h][:], in_=mic_v[g][:, :, h * W : (h + 1) * W])
+
+        def load_path(g):
+            nc.sync.dma_start(out=pbytes[g][:], in_=path_v[g])
+
+        def load_basis():
+            nc.sync.dma_start(out=bwords[:], in_=basis_words.rearrange("g p n -> p g n"))
+
+        def load_scales():
+            for q in range(4):
+                nc.sync.dma_start(
+                    out=bscale[32 * q : 32 * q + 4, :, :].bitcast(I32),
+                    in_=basis_scales[:, 4 * q : 4 * q + 4, :].bitcast(I32).rearrange("g q n -> q g n"),
+                )
+
+
+        steps = keep.tile([P, NG, PACK], F32, name="steps")
+        negstep = keep.tile([P, NG, PACK], F32, name="negstep")
+        gains = keep.tile([P, PACK], F32, name="gains")
+
+        def prep_steps():
+            nc.vector.tensor_copy(out=steps[:], in_=step_bf[:])
+            nc.vector.tensor_scalar(out=negstep[:], in0=step_bf[:], scalar1=-1.0, scalar2=None, op0=ALU.mult)
+
+        def prep_gains():
+            nc.vector.tensor_copy(out=gains[:], in_=gain_bf[:])
+
+
+        x_codes = [keep.tile([P, NK, PASS], U32, name=f"x_codes{g}", align_bytes=64) for g in range(NG)]
+        x_scales = [keep.tile([P, NK, PASS], U8, name=f"x_scales{g}", align_bytes=64) for g in range(NG)]
+        p_codes = [[keep.tile([P, W], U32, name=f"p_codes{g}_{h}", align_bytes=64) for h in range(NH)] for g in range(NK)]
+        p_scales = [[keep.tile([P, W], U8, name=f"p_scales{g}_{h}", align_bytes=64) for h in range(NH)] for g in range(NK)]
+        u_codes = [keep.tile([P, R], U32, name=f"u_codes{g}", align_bytes=64) for g in range(NG)]
+        u_scales = [keep.tile([P, R], U8, name=f"u_scales{g}", align_bytes=64) for g in range(NG)]
+        e_codes = [[keep.tile([P, W], U32, name=f"e_codes{g}_{h}", align_bytes=64) for h in range(NH)] for g in range(NG)]
+        e_scales = [[keep.tile([P, W], U8, name=f"e_scales{g}_{h}", align_bytes=64) for h in range(NH)] for g in range(NG)]
+
+        pwide = [[keep.tile([P, PACK, W], BF16, name=f"pwide{g}_{h}") for h in range(NH)] for g in range(NK)]
+        pil = {}
+
+        def widen_v(g, h, t):
+            nc.vector.tensor_scalar(
+                out=pwide[g][h][:, t, :],
+                in0=pbytes[g][:, t, h * W : (h + 1) * W].bitcast(FP8),
+                scalar1=pscale[:, g, t : t + 1],
+                scalar2=None,
+                op0=ALU.mult,
+            )
+
+        def widen(g, h, t):
+            nc.scalar.activation(
+                out=pwide[g][h][:, t, :],
+                in_=pbytes[g][:, t, h * W : (h + 1) * W].bitcast(FP8),
+                func=COPY,
+                scale=pscale[:, g, t : t + 1],
+            )
+
+        def path_il(g, h):
+            grouped = work.tile([P, W, PACK], BF16, name="p_grouped", align_bytes=64)
+            nc.vector.tensor_copy(
+                out=grouped[:].rearrange("p (c i) t -> p c t i", i=4),
+                in_=pwide[g][h][:].rearrange("p t (c i) -> p c t i", i=4),
+            )
+            pil[g, h] = grouped
+
+        def path_q(g, h):
+            nc.vector.quantize_mx(
+                out=p_codes[g][h][:].bitcast(FP8X4),
+                scales=p_scales[g][h][:],
+                in_=pil[g, h][:].rearrange("p c t -> p (c t)"),
+            )
+
+        xg = {}
+
+        xbank = {}
+
+        def far_turn(g, half, k):
+            words = far_t[g][:].bitcast(F32)
+            bank = turn.tile([P, 2, 2, P], F32, name="turn_bank")
+            for jj in range(2):
+                for u in range(2):
+                    nc.tensor.transpose(
+                        bank[:, jj, u, :], words[:, 2 * half + jj, 256 * k + u : 256 * (k + 1) : 2], ident[:]
+                    )
+            xbank[g, half, k] = bank
+
+        def far_copy(g, half, k):
+            if g not in xg:
+                xg[g] = work.tile([P, NK, PACK, P, 2], F32, name="x_grouped", align_bytes=64)
+            nc.scalar.copy(
+                out=xg[g][:, k, 2 * half : 2 * half + 2, :, :],
+                in_=xbank[g, half, k][:].rearrange("p j u n -> p j n u"),
+            )
+
+        def far_q(g, k, half=None):
+            lo, hi = (0, PASS) if half is None else (256 * half, 256 * half + 256)
+            flat = xg[g][:].rearrange("p k j n u -> p k (j n u)").bitcast(BF16)
+            nc.vector.quantize_mx(
+                out=x_codes[g][:, k, lo:hi].bitcast(FP8X4),
+                scales=x_scales[g][:, k, lo:hi],
+                in_=flat[:, k, 4 * lo : 4 * hi],
+            )
+
+        ug = {}
+
+        ubank = {}
+
+        def comp_mm(g, chunk):
+            bank = comp.tile([P, PACK, P], F32, name="comp_bank")
+            cols = slice(chunk * P, (chunk + 1) * P)
+            for j in range(PACK):
+                for k in range(NK):
+                    nc.tensor.matmul_mx(
+                        out=bank[:, j, :],
+                        lhsT=x_codes[g][:, k, j * P : (j + 1) * P].bitcast(FP8X4),
+                        lhsT_scale=x_scales[g][:, k, j * P : (j + 1) * P],
+                        rhs=bwords[:, k, 2 * chunk * P : 2 * (chunk + 1) * P].bitcast(FP4X4),
+                        rhs_scale=bscale[:, k, cols],
+                        start=(k == 0),
+                        stop=(k == NK - 1),
+                    )
+            ubank[g, chunk] = bank
+
+        def comp_copy(g, chunk):
+            if g not in ug:
+                ug[g] = work.tile([P, 4, P, PACK], BF16, name="u_grouped", align_bytes=64)
+            nc.scalar.copy(
+                out=ug[g][:, :, 32 * chunk : 32 * (chunk + 1), :],
+                in_=ubank[g, chunk][:].rearrange("p j (q m) -> p m q j", m=4),
+            )
+
+        def comp_q(g):
+            nc.vector.quantize_mx(
+                out=u_codes[g][:].bitcast(FP8X4),
+                scales=u_scales[g][:],
+                in_=ug[g][:].rearrange("p m q j -> p (m q j)"),
+            )
+
+        ms = {}
+        ep = {}
+        eg = {}
+        ebank = {}
+
+        def mic_scale_v(g, h, j):
+            if (g, h) not in ms:
+                ms[g, h] = work.tile([P, PACK, W], F32, name="mic_scaled", bufs=3)
+            nc.vector.tensor_scalar(
+                out=ms[g, h][:, j, :], in0=mic_t[g][h][:, j, :], scalar1=steps[:, g, j : j + 1], scalar2=None, op0=ALU.mult
+            )
+
+        def mic_scale(g, h, j):
+            if (g, h) not in ms:
+                ms[g, h] = work.tile([P, PACK, W], F32, name="mic_scaled", bufs=3)
+            nc.scalar.activation(
+                out=ms[g, h][:, j, :], in_=mic_t[g][h][:, j, :], func=COPY, scale=steps[:, g, j : j + 1]
+            )
+
+        def echo_mm(g, h, j):
+            bank = echo.tile([P, W], F32, name="echo_bank")
+            for k in range(NK):
+                nc.tensor.matmul_mx(
+                    out=bank[:],
+                    lhsT=x_codes[g][:, k, j * P : (j + 1) * P].bitcast(FP8X4),
+                    lhsT_scale=x_scales[g][:, k, j * P : (j + 1) * P],
+                    rhs=p_codes[k][h][:].bitcast(FP8X4),
+                    rhs_scale=p_scales[k][h][:],
+                    start=(k == 0),
+                    stop=(k == NK - 1),
+                )
+            ebank[g, h, j] = bank
+
+        def err(g, h, j):
+            if (g, h) not in ep:
+                ep[g, h] = work.tile([P, PACK, W], BF16, name="e_rows", bufs=3)
+            nc.vector.scalar_tensor_tensor(
+                out=ep[g, h][:, j, :],
+                in0=ebank[g, h, j][:],
+                scalar=negstep[:, g, j : j + 1],
+                in1=ms[g, h][:, j, :],
+                op0=ALU.mult,
+                op1=ALU.add,
+            )
+
+        def err_il(g, h, lo, hi):
+            if (g, h) not in eg:
+                eg[g, h] = work.tile([P, W, PACK], BF16, name="e_grouped", align_bytes=64)
+            nc.vector.tensor_copy(
+                out=eg[g, h][:, lo:hi, :].rearrange("p (c i) j -> p c j i", i=4),
+                in_=ep[g, h][:, :, lo:hi].rearrange("p j (c i) -> p c j i", i=4),
+            )
+
+        def err_il_s(g, h, lo, hi):
+            if (g, h) not in eg:
+                eg[g, h] = work.tile([P, W, PACK], BF16, name="e_grouped", align_bytes=64)
+            nc.scalar.copy(
+                out=eg[g, h][:, lo:hi, :].rearrange("p (c i) j -> p c j i", i=4),
+                in_=ep[g, h][:, :, lo:hi].rearrange("p j (c i) -> p c j i", i=4),
+            )
+
+        def err_q(g, h, lo=0, hi=W):
+            nc.vector.quantize_mx(
+                out=e_codes[g][h][:, lo:hi].bitcast(FP8X4),
+                scales=e_scales[g][h][:, lo:hi],
+                in_=eg[g, h][:, lo:hi, :].rearrange("p c j -> p (c j)"),
+            )
+
+        out_v = out.rearrange("(q m) c -> m q c", m=4)
+
+        def grad_mm(bank, g, h, m):
+            nc.tensor.matmul_mx(
+                out=bank[:],
+                lhsT=u_codes[g][:, m * P : (m + 1) * P].bitcast(FP8X4),
+                lhsT_scale=u_scales[g][:, m * P : (m + 1) * P],
+                rhs=e_codes[g][h][:].bitcast(FP8X4),
+                rhs_scale=e_scales[g][h][:],
+                start=(g == 0),
+                stop=(g == NG - 1),
+            )
+
+        gbank = {}
+
+        def grad0(m):
+            bank = comp.tile([P, W], F32, name="comp_bank")
+            for g in range(NG):
+                grad_mm(bank, g, 0, m)
+            gbank[0, m] = bank
+
+        def grad1(m):
+            if m < 2:
+                bank = turn.tile([P, W], F32, name="turn_bank")
+            else:
+                bank = comp.tile([P, W], F32, name="comp_bank")
+            for g in range(NG - 1):
+                grad_mm(bank, g, 1, m)
+            gbank[1, m] = bank
+
+        def grad2(m):
+            grad_mm(gbank[1, m], NG - 1, 1, m)
+
+        def out_s(h, m):
+            res = work.tile([P, W], F32, name="res", bufs=4)
+            nc.scalar.activation(out=res[:], in_=gbank[h, m][:], func=COPY, scale=gains[:, m : m + 1])
+            nc.sync.dma_start(out=out_v[m][:, h * W : (h + 1) * W], in_=res[:])
+
+        def out_v_(h, m):
+            res = work.tile([P, W], F32, name="res", bufs=4)
+            nc.vector.tensor_scalar(
+                out=res[:], in0=gbank[h, m][:], scalar1=gains[:, m : m + 1], scalar2=None, op0=ALU.mult
+            )
+            nc.sync.dma_start(out=out_v[m][:, h * W : (h + 1) * W], in_=res[:])
+
+        ctx.enter_context(tc.manual_schedule())
+        load_path(0)
+        load_far(0, 0)
+        load_path(1)
+        load_far(0, 1)
+        load_far(1, 1)
+        load_basis()
+        load_mic(0, 0)
+        load_scales()
+        load_mic(3, 1)
+        load_mic(1, 0)
+        load_mic(2, 0)
+        load_far(1, 0)
+        load_far(2, 0)
+        load_far(2, 1)
+        load_mic(0, 1)
+        load_far(3, 0)
+        load_mic(3, 0)
+        load_far(3, 1)
+        load_mic(2, 1)
+        load_mic(1, 1)
+        widen_v(0, 0, 1)
+        widen(0, 1, 1)
+        widen_v(0, 1, 2)
+        widen(0, 1, 3)
+        widen_v(0, 0, 3)
+        widen_v(0, 1, 0)
+        widen(0, 0, 0)
+        far_turn(0, 0, 1)
+        widen_v(0, 0, 2)
+        prep_gains()
+        far_turn(0, 0, 0)
+        far_copy(0, 0, 1)
+        widen_v(1, 0, 1)
+        far_copy(0, 0, 0)
+        prep_steps()
+        path_il(0, 0)
+        widen(1, 1, 1)
+        far_turn(0, 1, 0)
+        widen(1, 1, 0)
+        far_turn(0, 1, 1)
+        path_q(0, 0)
+        far_copy(0, 1, 0)
+        widen_v(1, 0, 3)
+        far_copy(0, 1, 1)
+        far_q(0, 0, None)
+        far_turn(1, 1, 1)
+        widen(1, 0, 0)
+        far_turn(1, 1, 0)
+        far_q(0, 1, None)
+        far_copy(1, 1, 1)
+        comp_mm(0, 0)
+        widen_v(1, 0, 2)
+        mic_scale(0, 0, 1)
+        path_il(1, 0)
+        comp_mm(0, 2)
+        comp_copy(0, 0)
+        mic_scale(0, 0, 3)
+        path_q(1, 0)
+        comp_mm(0, 1)
+        far_copy(1, 1, 0)
+        widen_v(1, 1, 2)
+        echo_mm(0, 0, 3)
+        mic_scale_v(1, 0, 2)
+        mic_scale(0, 0, 0)
+        mic_scale_v(1, 0, 1)
+        echo_mm(0, 0, 1)
+        mic_scale_v(0, 0, 2)
+        comp_copy(0, 1)
+        err(0, 0, 3)
+        echo_mm(0, 0, 0)
+        comp_copy(0, 2)
+        err(0, 0, 1)
+        echo_mm(0, 0, 2)
+        mic_scale(2, 0, 3)
+        err(0, 0, 0)
+        far_turn(1, 0, 1)
+        widen(1, 1, 3)
+        err(0, 0, 2)
+        far_turn(1, 0, 0)
+        far_copy(1, 0, 1)
+        comp_mm(0, 3)
+        err_il(0, 0, 0, 416)
+        far_copy(1, 0, 0)
+        far_turn(2, 0, 0)
+        mic_scale(1, 0, 0)
+        path_il(1, 1)
+        far_turn(2, 0, 1)
+        far_copy(2, 0, 0)
+        far_q(1, 1, None)
+        far_copy(2, 0, 1)
+        far_turn(2, 1, 1)
+        far_q(1, 0, None)
+        comp_copy(0, 3)
+        far_turn(2, 1, 0)
+        path_il(0, 1)
+        err_il_s(0, 0, 416, 512)
+        echo_mm(1, 0, 0)
+        far_copy(2, 1, 1)
+        comp_mm(1, 0)
+        far_copy(2, 1, 0)
+        path_q(0, 1)
+        mic_scale(2, 0, 0)
+        echo_mm(1, 0, 2)
+        err_q(0, 0, 0, 512)
+        comp_copy(1, 0)
+        comp_mm(1, 1)
+        far_q(2, 0, None)
+        mic_scale(2, 0, 2)
+        echo_mm(1, 0, 3)
+        err(1, 0, 2)
+        mic_scale(1, 0, 3)
+        echo_mm(1, 0, 1)
+        far_q(2, 1, None)
+        mic_scale(0, 1, 1)
+        far_turn(3, 0, 1)
+        err(1, 0, 0)
+        mic_scale(0, 1, 0)
+        far_turn(3, 0, 0)
+        err(1, 0, 3)
+        mic_scale(0, 1, 2)
+        echo_mm(2, 0, 1)
+        err(1, 0, 1)
+        far_copy(3, 0, 1)
+        comp_mm(1, 2)
+        err_il(1, 0, 0, 416)
+        far_copy(3, 0, 0)
+        echo_mm(2, 0, 0)
+        mic_scale(3, 0, 3)
+        comp_q(0)
+        echo_mm(2, 0, 2)
+        err_il_s(1, 0, 416, 512)
+        path_q(1, 1)
+        mic_scale(2, 0, 1)
+        far_turn(3, 1, 0)
+        err_q(1, 0, 0, 512)
+        comp_copy(1, 1)
+        far_turn(3, 1, 1)
+        err(2, 0, 1)
+        echo_mm(0, 1, 0)
+        comp_copy(1, 2)
+        err(2, 0, 0)
+        mic_scale(0, 1, 3)
+        echo_mm(2, 0, 3)
+        err(2, 0, 2)
+        far_copy(3, 1, 1)
+        comp_mm(1, 3)
+        err(0, 1, 0)
+        far_copy(3, 1, 0)
+        echo_mm(0, 1, 1)
+        err(2, 0, 3)
+        comp_copy(1, 3)
+        comp_mm(2, 0)
+        far_q(3, 0, None)
+        mic_scale(1, 1, 3)
+        echo_mm(0, 1, 3)
+        err(0, 1, 1)
+        mic_scale(1, 1, 1)
+        comp_mm(2, 1)
+        err_il(2, 0, 0, 416)
+        comp_copy(2, 0)
+        echo_mm(0, 1, 2)
+        err(0, 1, 3)
+        comp_copy(2, 1)
+        comp_mm(2, 2)
+        far_q(3, 1, None)
+        echo_mm(3, 0, 0)
+        comp_copy(2, 2)
+        err(0, 1, 2)
+        echo_mm(3, 0, 2)
+        err_il_s(2, 0, 416, 512)
+        comp_q(1)
+        mic_scale(3, 0, 0)
+        echo_mm(3, 0, 1)
+        err_q(2, 0, 0, 512)
+        mic_scale(3, 0, 2)
+        comp_mm(3, 0)
+        err(3, 0, 0)
+        mic_scale(3, 0, 1)
+        echo_mm(3, 0, 3)
+        err(3, 0, 2)
+        mic_scale(1, 1, 2)
+        comp_mm(3, 1)
+        err(3, 0, 1)
+        comp_copy(3, 0)
+        err(3, 0, 3)
+        echo_mm(1, 1, 1)
+        mic_scale(3, 1, 1)
+        echo_mm(2, 1, 3)
+        err_il(3, 0, 0, 416)
+        err_il_s(3, 0, 416, 512)
+        echo_mm(2, 1, 0)
+        err_il_s(0, 1, 416, 512)
+        comp_copy(3, 1)
+        err_il(0, 1, 0, 416)
+        comp_mm(2, 3)
+        mic_scale(2, 1, 3)
+        comp_mm(3, 3)
+        err(1, 1, 1)
+        mic_scale(2, 1, 0)
+        echo_mm(1, 1, 3)
+        err(2, 1, 3)
+        comp_copy(2, 3)
+        echo_mm(3, 1, 0)
+        err(2, 1, 0)
+        mic_scale(1, 1, 0)
+        echo_mm(1, 1, 2)
+        comp_q(2)
+        mic_scale(2, 1, 2)
+        echo_mm(2, 1, 2)
+        err(1, 1, 3)
+        mic_scale(3, 1, 0)
+        comp_mm(3, 2)
+        err(1, 1, 2)
+        mic_scale(3, 1, 2)
+        echo_mm(1, 1, 0)
+        err(3, 1, 0)
+        mic_scale(2, 1, 1)
+        err(2, 1, 2)
+        comp_copy(3, 2)
+        echo_mm(3, 1, 2)
+        err(1, 1, 0)
+        echo_mm(2, 1, 1)
+        comp_copy(3, 3)
+        err(3, 1, 2)
+        echo_mm(3, 1, 3)
+        err_q(3, 0, 0, 512)
+        comp_q(3)
+        grad0(3)
+        err_il_s(1, 1, 416, 512)
+        err_q(0, 1, 0, 512)
+        mic_scale(3, 1, 3)
+        grad0(2)
+        err(2, 1, 1)
+        out_s(0, 3)
+        err_il(1, 1, 0, 416)
+        err_il_s(2, 1, 416, 512)
+        grad0(1)
+        out_s(0, 2)
+        err_il(2, 1, 0, 416)
+        echo_mm(3, 1, 1)
+        err_q(1, 1, 0, 512)
+        out_s(0, 1)
+        grad0(0)
+        err(3, 1, 3)
+        err_q(2, 1, 0, 512)
+        grad1(3)
+        err(3, 1, 1)
+        out_s(0, 0)
+        grad1(0)
+        err_il(3, 1, 0, 416)
+        err_il_s(3, 1, 416, 512)
+        grad1(2)
+        err_q(3, 1, 0, 512)
+        grad2(3)
+        grad2(2)
+        out_v_(1, 3)
+        grad2(0)
+        out_s(1, 2)
+        grad1(1)
+        out_s(1, 0)
+        grad2(1)
+        out_v_(1, 1)

@@ -33,19 +33,18 @@ def tile_echo_nlms_gradient_s11_kernel(
     with ExitStack() as ctx:
         keep = ctx.enter_context(tc.tile_pool(name="keep", bufs=1))
         work = ctx.enter_context(tc.tile_pool(name="work", bufs=2))
-        turn = ctx.enter_context(tc.psum_pool(name="turn", bufs=2))
+        turn = ctx.enter_context(tc.psum_pool(name="turn", bufs=3))
         comp = ctx.enter_context(tc.psum_pool(name="comp", bufs=2))
-        echo = ctx.enter_context(tc.psum_pool(name="echo", bufs=4))
-
-        pscale = keep.tile([P, NK, PACK], F32, name="pscale")
-        nc.scalar.dma_start(out=pscale[:], in_=path_scale.rearrange("(g p t) o -> p g (t o)", p=P, t=PACK))
-        step_bf = keep.tile([P, NG, PACK], BF16, name="step_bf")
-        nc.gpsimd.dma_start(out=step_bf[:], in_=step.rearrange("(g p j) -> p g j", p=P, j=PACK))
-        gain_bf = keep.tile([P, PACK], BF16, name="gain_bf")
-        nc.gpsimd.dma_start(out=gain_bf[:], in_=gain.rearrange("(q m) -> q m", m=PACK))
+        echo = ctx.enter_context(tc.psum_pool(name="echo", bufs=3))
 
         ident = keep.tile([P, P], F32, name="ident")
         make_identity(nc, ident[:])
+        pscale = keep.tile([P, NK, PACK], F32, name="pscale")
+        nc.scalar.dma_start(out=pscale[:], in_=path_scale.rearrange("(g p t) o -> p g (t o)", p=P, t=PACK))
+        step_bf = keep.tile([P, NG, PACK], BF16, name="step_bf")
+        nc.scalar.dma_start(out=step_bf[:], in_=step.rearrange("(g p j) -> p g j", p=P, j=PACK))
+        gain_bf = keep.tile([P, PACK], BF16, name="gain_bf")
+        nc.scalar.dma_start(out=gain_bf[:], in_=gain.rearrange("(q m) -> q m", m=PACK))
         bscale = keep.tile([P, NK, R], U8, name="bscale", align_bytes=64)
         nc.vector.memset(bscale[:].rearrange("p g n -> p (g n)").bitcast(I32), 0)
 
@@ -57,15 +56,15 @@ def tile_echo_nlms_gradient_s11_kernel(
         mic_v = mic.rearrange("(g p j) c -> g p j c", p=P, j=PACK)
         path_v = path_bytes.rearrange("(g p t) c -> g p t c", p=P, t=PACK)
 
-        def load_far(g, half):
-            js = slice(2 * half, 2 * half + 2)
-            nc.sync.dma_start(out=far_t[g][:, js, :], in_=far_v[g][:, js, :])
+        def load_far(g, lo, hi):
+            nc.sync.dma_start(out=far_t[g][:, lo:hi, :], in_=far_v[g][:, lo:hi, :])
 
         def load_mic(g, h):
             nc.sync.dma_start(out=mic_t[g][h][:], in_=mic_v[g][:, :, h * W : (h + 1) * W])
 
-        def load_path(g):
-            nc.sync.dma_start(out=pbytes[g][:], in_=path_v[g])
+        def load_path(g, half):
+            ts = slice(2 * half, 2 * half + 2)
+            nc.sync.dma_start(out=pbytes[g][:, ts, :], in_=path_v[g][:, ts, :])
 
         def load_basis():
             nc.sync.dma_start(out=bwords[:], in_=basis_words.rearrange("g p n -> p g n"))
@@ -83,11 +82,11 @@ def tile_echo_nlms_gradient_s11_kernel(
         gains = keep.tile([P, PACK], F32, name="gains")
 
         def prep_steps():
-            nc.vector.tensor_copy(out=steps[:], in_=step_bf[:])
-            nc.vector.tensor_scalar(out=negstep[:], in0=step_bf[:], scalar1=-1.0, scalar2=None, op0=ALU.mult)
+            nc.gpsimd.tensor_copy(out=steps[:], in_=step_bf[:])
+            nc.gpsimd.tensor_scalar(out=negstep[:], in0=step_bf[:], scalar1=-1.0, scalar2=0.0, op0=ALU.mult, op1=ALU.add)
 
         def prep_gains():
-            nc.vector.tensor_copy(out=gains[:], in_=gain_bf[:])
+            nc.gpsimd.tensor_copy(out=gains[:], in_=gain_bf[:])
 
 
         x_codes = [keep.tile([P, NK, PASS], U32, name=f"x_codes{g}", align_bytes=64) for g in range(NG)]
@@ -120,12 +119,18 @@ def tile_echo_nlms_gradient_s11_kernel(
             )
 
         def path_il(g, h):
-            grouped = work.tile([P, W, PACK], BF16, name="p_grouped", align_bytes=64)
+            pil[g, h] = work.tile([P, W, PACK], BF16, name="p_grouped", align_bytes=64)
             nc.vector.tensor_copy(
-                out=grouped[:].rearrange("p (c i) t -> p c t i", i=4),
+                out=pil[g, h][:].rearrange("p (c i) t -> p c t i", i=4),
                 in_=pwide[g][h][:].rearrange("p t (c i) -> p c t i", i=4),
             )
-            pil[g, h] = grouped
+
+        def path_il_s(g, h):
+            pil[g, h] = work.tile([P, W, PACK], BF16, name="p_grouped", align_bytes=64)
+            nc.scalar.copy(
+                out=pil[g, h][:].rearrange("p (c i) t -> p c t i", i=4),
+                in_=pwide[g][h][:].rearrange("p t (c i) -> p c t i", i=4),
+            )
 
         def path_q(g, h):
             nc.vector.quantize_mx(
@@ -156,13 +161,17 @@ def tile_echo_nlms_gradient_s11_kernel(
                 in_=xbank[g, half, k][:].rearrange("p j u n -> p j n u"),
             )
 
-        def far_q(g, k, half=None):
-            lo, hi = (0, PASS) if half is None else (256 * half, 256 * half + 256)
+        def far_q(g, k):
             flat = xg[g][:].rearrange("p k j n u -> p k (j n u)").bitcast(BF16)
             nc.vector.quantize_mx(
-                out=x_codes[g][:, k, lo:hi].bitcast(FP8X4),
-                scales=x_scales[g][:, k, lo:hi],
-                in_=flat[:, k, 4 * lo : 4 * hi],
+                out=x_codes[g][:, k, :].bitcast(FP8X4), scales=x_scales[g][:, k, :], in_=flat[:, k, :]
+            )
+
+        def far_q2(g):
+            nc.vector.quantize_mx(
+                out=x_codes[g][:].rearrange("p k n -> p (k n)").bitcast(FP8X4),
+                scales=x_scales[g][:].rearrange("p k n -> p (k n)"),
+                in_=xg[g][:].rearrange("p k j n u -> p (k j n u)").bitcast(BF16),
             )
 
         ug = {}
@@ -210,6 +219,18 @@ def tile_echo_nlms_gradient_s11_kernel(
                 ms[g, h] = work.tile([P, PACK, W], F32, name="mic_scaled", bufs=3)
             nc.vector.tensor_scalar(
                 out=ms[g, h][:, j, :], in0=mic_t[g][h][:, j, :], scalar1=steps[:, g, j : j + 1], scalar2=None, op0=ALU.mult
+            )
+
+        def mic_scale_g(g, h, j):
+            if (g, h) not in ms:
+                ms[g, h] = work.tile([P, PACK, W], F32, name="mic_scaled", bufs=3)
+            nc.gpsimd.tensor_scalar(
+                out=ms[g, h][:, j, :],
+                in0=mic_t[g][h][:, j, :],
+                scalar1=steps[:, g, j : j + 1],
+                scalar2=0.0,
+                op0=ALU.mult,
+                op1=ALU.add,
             )
 
         def mic_scale(g, h, j):
@@ -314,265 +335,264 @@ def tile_echo_nlms_gradient_s11_kernel(
             nc.sync.dma_start(out=out_v[m][:, h * W : (h + 1) * W], in_=res[:])
 
         ctx.enter_context(tc.manual_schedule())
-        load_path(0)
-        load_far(0, 0)
-        load_path(1)
-        load_far(0, 1)
-        load_far(1, 1)
+        load_path(0, 0)
+        load_path(1, 1)
+        load_path(0, 1)
+        load_path(1, 0)
+        load_far(0, 0, 2)
+        load_far(0, 2, 4)
+        load_far(1, 2, 4)
+        load_far(1, 0, 2)
+        load_far(2, 2, 4)
+        load_far(2, 0, 2)
+        load_mic(1, 0)
+        load_far(3, 0, 2)
+        load_mic(3, 1)
+        load_mic(2, 0)
         load_basis()
         load_mic(0, 0)
         load_scales()
-        load_mic(3, 1)
-        load_mic(1, 0)
-        load_mic(2, 0)
-        load_far(1, 0)
-        load_far(2, 0)
-        load_far(2, 1)
-        load_mic(0, 1)
-        load_far(3, 0)
-        load_mic(3, 0)
-        load_far(3, 1)
-        load_mic(2, 1)
+        load_far(3, 2, 4)
         load_mic(1, 1)
+        load_mic(3, 0)
+        load_mic(2, 1)
+        load_mic(0, 1)
+        widen(0, 0, 0)
+        widen_v(0, 1, 0)
         widen_v(0, 0, 1)
         widen(0, 1, 1)
-        widen_v(0, 1, 2)
-        widen(0, 1, 3)
-        widen_v(0, 0, 3)
-        widen_v(0, 1, 0)
-        widen(0, 0, 0)
-        far_turn(0, 0, 1)
-        widen_v(0, 0, 2)
-        prep_gains()
-        far_turn(0, 0, 0)
-        far_copy(0, 0, 1)
-        widen_v(1, 0, 1)
-        far_copy(0, 0, 0)
-        prep_steps()
-        path_il(0, 0)
-        widen(1, 1, 1)
-        far_turn(0, 1, 0)
-        widen(1, 1, 0)
-        far_turn(0, 1, 1)
-        path_q(0, 0)
-        far_copy(0, 1, 0)
-        widen_v(1, 0, 3)
-        far_copy(0, 1, 1)
-        far_q(0, 0, None)
-        far_turn(1, 1, 1)
-        widen(1, 0, 0)
-        far_turn(1, 1, 0)
-        far_q(0, 1, None)
-        far_copy(1, 1, 1)
-        comp_mm(0, 0)
+        widen(1, 1, 3)
         widen_v(1, 0, 2)
-        mic_scale(0, 0, 1)
+        widen_v(0, 1, 3)
+        widen_v(0, 0, 3)
+        widen_v(0, 1, 2)
+        widen(1, 0, 3)
+        widen_v(1, 0, 0)
+        widen_v(1, 0, 1)
+        prep_gains()
+        widen(1, 1, 1)
+        widen(1, 1, 2)
+        widen(1, 1, 0)
+        widen_v(0, 0, 2)
+        far_turn(0, 0, 0)
+        far_turn(0, 0, 1)
+        far_turn(0, 1, 1)
         path_il(1, 0)
-        comp_mm(0, 2)
-        comp_copy(0, 0)
-        mic_scale(0, 0, 3)
+        far_copy(0, 0, 0)
+        far_turn(0, 1, 0)
+        path_il(0, 0)
+        far_turn(1, 1, 0)
         path_q(1, 0)
-        comp_mm(0, 1)
+        far_copy(0, 0, 1)
+        far_copy(0, 1, 1)
+        far_q(0, 1)
+        far_copy(0, 1, 0)
+        far_q(0, 0)
+        path_q(0, 0)
         far_copy(1, 1, 0)
-        widen_v(1, 1, 2)
-        echo_mm(0, 0, 3)
-        mic_scale_v(1, 0, 2)
-        mic_scale(0, 0, 0)
-        mic_scale_v(1, 0, 1)
-        echo_mm(0, 0, 1)
+        far_turn(1, 1, 1)
+        far_copy(1, 1, 1)
+        far_turn(1, 0, 0)
+        far_copy(1, 0, 0)
+        far_turn(1, 0, 1)
+        far_turn(2, 1, 0)
+        path_il(1, 1)
+        prep_steps()
+        far_copy(1, 0, 1)
+        far_q2(1)
+        far_turn(2, 1, 1)
+        far_turn(2, 0, 0)
+        far_copy(2, 1, 0)
+        far_turn(2, 0, 1)
+        path_q(1, 1)
+        far_copy(2, 1, 1)
+        far_copy(2, 0, 0)
+        path_il(0, 1)
+        echo_mm(1, 0, 1)
+        far_copy(2, 0, 1)
+        far_q2(2)
+        mic_scale(1, 0, 2)
+        echo_mm(1, 0, 2)
+        mic_scale(1, 0, 0)
+        err(1, 0, 2)
+        mic_scale(1, 0, 1)
+        mic_scale(1, 0, 3)
+        far_turn(3, 0, 1)
+        far_copy(3, 0, 1)
+        far_turn(3, 0, 0)
+        mic_scale(2, 0, 3)
+        echo_mm(1, 0, 0)
+        comp_mm(0, 0)
+        err(1, 0, 1)
+        err(1, 0, 0)
+        mic_scale(2, 0, 1)
         mic_scale_v(0, 0, 2)
+        comp_copy(0, 0)
+        path_q(0, 1)
+        comp_mm(0, 1)
+        mic_scale_v(0, 0, 3)
+        echo_mm(1, 0, 3)
+        err(1, 0, 3)
+        mic_scale(2, 0, 0)
+        echo_mm(0, 0, 3)
         comp_copy(0, 1)
         err(0, 0, 3)
-        echo_mm(0, 0, 0)
-        comp_copy(0, 2)
-        err(0, 0, 1)
         echo_mm(0, 0, 2)
-        mic_scale(2, 0, 3)
-        err(0, 0, 0)
-        far_turn(1, 0, 1)
-        widen(1, 1, 3)
         err(0, 0, 2)
-        far_turn(1, 0, 0)
-        far_copy(1, 0, 1)
-        comp_mm(0, 3)
-        err_il(0, 0, 0, 416)
-        far_copy(1, 0, 0)
-        far_turn(2, 0, 0)
-        mic_scale(1, 0, 0)
-        path_il(1, 1)
-        far_turn(2, 0, 1)
-        far_copy(2, 0, 0)
-        far_q(1, 1, None)
-        far_copy(2, 0, 1)
-        far_turn(2, 1, 1)
-        far_q(1, 0, None)
-        comp_copy(0, 3)
-        far_turn(2, 1, 0)
-        path_il(0, 1)
-        err_il_s(0, 0, 416, 512)
-        echo_mm(1, 0, 0)
-        far_copy(2, 1, 1)
-        comp_mm(1, 0)
-        far_copy(2, 1, 0)
-        path_q(0, 1)
-        mic_scale(2, 0, 0)
-        echo_mm(1, 0, 2)
-        err_q(0, 0, 0, 512)
-        comp_copy(1, 0)
-        comp_mm(1, 1)
-        far_q(2, 0, None)
-        mic_scale(2, 0, 2)
-        echo_mm(1, 0, 3)
-        err(1, 0, 2)
-        mic_scale(1, 0, 3)
-        echo_mm(1, 0, 1)
-        far_q(2, 1, None)
-        mic_scale(0, 1, 1)
-        far_turn(3, 0, 1)
-        err(1, 0, 0)
-        mic_scale(0, 1, 0)
-        far_turn(3, 0, 0)
-        err(1, 0, 3)
-        mic_scale(0, 1, 2)
-        echo_mm(2, 0, 1)
-        err(1, 0, 1)
-        far_copy(3, 0, 1)
-        comp_mm(1, 2)
-        err_il(1, 0, 0, 416)
-        far_copy(3, 0, 0)
-        echo_mm(2, 0, 0)
-        mic_scale(3, 0, 3)
-        comp_q(0)
-        echo_mm(2, 0, 2)
-        err_il_s(1, 0, 416, 512)
-        path_q(1, 1)
-        mic_scale(2, 0, 1)
-        far_turn(3, 1, 0)
-        err_q(1, 0, 0, 512)
-        comp_copy(1, 1)
         far_turn(3, 1, 1)
-        err(2, 0, 1)
-        echo_mm(0, 1, 0)
-        comp_copy(1, 2)
-        err(2, 0, 0)
-        mic_scale(0, 1, 3)
-        echo_mm(2, 0, 3)
-        err(2, 0, 2)
+        far_turn(3, 1, 0)
+        err_il(1, 0, 0, 320)
+        far_copy(3, 0, 0)
+        mic_scale(0, 0, 1)
         far_copy(3, 1, 1)
-        comp_mm(1, 3)
-        err(0, 1, 0)
-        far_copy(3, 1, 0)
-        echo_mm(0, 1, 1)
-        err(2, 0, 3)
-        comp_copy(1, 3)
         comp_mm(2, 0)
-        far_q(3, 0, None)
-        mic_scale(1, 1, 3)
-        echo_mm(0, 1, 3)
-        err(0, 1, 1)
-        mic_scale(1, 1, 1)
-        comp_mm(2, 1)
-        err_il(2, 0, 0, 416)
+        comp_mm(0, 2)
+        mic_scale_v(3, 0, 3)
+        echo_mm(0, 0, 1)
+        far_copy(3, 1, 0)
+        far_q2(3)
+        echo_mm(0, 0, 0)
+        mic_scale(0, 0, 0)
+        comp_copy(0, 2)
         comp_copy(2, 0)
-        echo_mm(0, 1, 2)
-        err(0, 1, 3)
-        comp_copy(2, 1)
-        comp_mm(2, 2)
-        far_q(3, 1, None)
-        echo_mm(3, 0, 0)
-        comp_copy(2, 2)
-        err(0, 1, 2)
-        echo_mm(3, 0, 2)
-        err_il_s(2, 0, 416, 512)
-        comp_q(1)
-        mic_scale(3, 0, 0)
-        echo_mm(3, 0, 1)
-        err_q(2, 0, 0, 512)
-        mic_scale(3, 0, 2)
-        comp_mm(3, 0)
-        err(3, 0, 0)
+        echo_mm(2, 0, 0)
+        comp_mm(0, 3)
+        err(0, 0, 1)
+        err_il_s(1, 0, 320, 512)
         mic_scale(3, 0, 1)
-        echo_mm(3, 0, 3)
+        echo_mm(2, 0, 3)
+        err(0, 0, 0)
+        err(2, 0, 0)
+        comp_copy(0, 3)
+        err_il_s(0, 0, 352, 512)
+        echo_mm(2, 0, 1)
+        err_q(1, 0, 0, 512)
+        mic_scale(2, 0, 2)
+        comp_mm(2, 1)
+        echo_mm(2, 0, 2)
+        comp_copy(2, 1)
+        err(2, 0, 3)
+        comp_mm(1, 0)
+        echo_mm(3, 0, 2)
+        comp_q(0)
+        mic_scale(3, 0, 2)
+        err(2, 0, 1)
+        comp_copy(1, 0)
+        mic_scale(0, 1, 3)
+        comp_mm(1, 1)
+        comp_copy(1, 1)
+        err(2, 0, 2)
+        err_il(0, 0, 0, 352)
+        echo_mm(0, 1, 3)
+        comp_mm(2, 2)
+        echo_mm(3, 0, 0)
+        err_il(2, 0, 0, 416)
+        mic_scale(0, 1, 0)
         err(3, 0, 2)
-        mic_scale(1, 1, 2)
-        comp_mm(3, 1)
-        err(3, 0, 1)
-        comp_copy(3, 0)
-        err(3, 0, 3)
-        echo_mm(1, 1, 1)
-        mic_scale(3, 1, 1)
-        echo_mm(2, 1, 3)
-        err_il(3, 0, 0, 416)
-        err_il_s(3, 0, 416, 512)
-        echo_mm(2, 1, 0)
-        err_il_s(0, 1, 416, 512)
-        comp_copy(3, 1)
-        err_il(0, 1, 0, 416)
         comp_mm(2, 3)
-        mic_scale(2, 1, 3)
-        comp_mm(3, 3)
-        err(1, 1, 1)
-        mic_scale(2, 1, 0)
-        echo_mm(1, 1, 3)
-        err(2, 1, 3)
+        err(0, 1, 3)
+        comp_copy(2, 2)
+        mic_scale_v(3, 0, 0)
+        echo_mm(3, 0, 1)
+        comp_mm(3, 0)
+        mic_scale(0, 1, 1)
+        err_q(0, 0, 0, 512)
+        err(3, 0, 0)
+        echo_mm(0, 1, 1)
         comp_copy(2, 3)
-        echo_mm(3, 1, 0)
-        err(2, 1, 0)
-        mic_scale(1, 1, 0)
-        echo_mm(1, 1, 2)
         comp_q(2)
-        mic_scale(2, 1, 2)
-        echo_mm(2, 1, 2)
-        err(1, 1, 3)
-        mic_scale(3, 1, 0)
-        comp_mm(3, 2)
+        err_il_s(2, 0, 416, 512)
+        mic_scale(1, 1, 2)
+        comp_mm(1, 2)
+        mic_scale(0, 1, 2)
+        err(3, 0, 1)
+        err_q(2, 0, 0, 512)
+        echo_mm(3, 0, 3)
+        comp_copy(3, 0)
+        echo_mm(1, 1, 2)
+        comp_mm(3, 1)
+        err(0, 1, 1)
+        comp_copy(1, 2)
+        mic_scale(1, 1, 1)
+        err(3, 0, 3)
         err(1, 1, 2)
-        mic_scale(3, 1, 2)
+        comp_mm(1, 3)
+        mic_scale(1, 1, 0)
+        comp_copy(3, 1)
+        echo_mm(0, 1, 0)
+        err_il(3, 0, 0, 320)
+        echo_mm(0, 1, 2)
+        err(0, 1, 0)
         echo_mm(1, 1, 0)
-        err(3, 1, 0)
-        mic_scale(2, 1, 1)
-        err(2, 1, 2)
-        comp_copy(3, 2)
-        echo_mm(3, 1, 2)
+        comp_copy(1, 3)
+        comp_mm(3, 2)
+        err(0, 1, 2)
+        comp_q(1)
+        comp_mm(3, 3)
+        mic_scale(2, 1, 2)
+        err_il_s(3, 0, 320, 512)
+        echo_mm(2, 1, 0)
+        mic_scale(2, 1, 0)
+        echo_mm(2, 1, 2)
         err(1, 1, 0)
         echo_mm(2, 1, 1)
-        comp_copy(3, 3)
-        err(3, 1, 2)
-        echo_mm(3, 1, 3)
+        comp_copy(3, 2)
         err_q(3, 0, 0, 512)
-        comp_q(3)
-        grad0(3)
-        err_il_s(1, 1, 416, 512)
-        err_q(0, 1, 0, 512)
-        mic_scale(3, 1, 3)
-        grad0(2)
+        err(2, 1, 0)
+        mic_scale(2, 1, 1)
+        comp_copy(3, 3)
+        echo_mm(2, 1, 3)
+        err(2, 1, 2)
+        echo_mm(1, 1, 3)
+        mic_scale(2, 1, 3)
         err(2, 1, 1)
-        out_s(0, 3)
-        err_il(1, 1, 0, 416)
-        err_il_s(2, 1, 416, 512)
+        echo_mm(1, 1, 1)
+        err_il_s(0, 1, 256, 512)
+        mic_scale(1, 1, 3)
+        comp_q(3)
+        grad0(2)
+        err(2, 1, 3)
+        err_il_s(2, 1, 256, 512)
+        err_il(0, 1, 0, 256)
+        err_il(2, 1, 0, 256)
+        echo_mm(3, 1, 3)
+        mic_scale(3, 1, 3)
+        grad0(0)
+        err(1, 1, 1)
+        mic_scale(3, 1, 0)
+        echo_mm(3, 1, 0)
+        echo_mm(3, 1, 1)
         grad0(1)
         out_s(0, 2)
-        err_il(2, 1, 0, 416)
-        echo_mm(3, 1, 1)
-        err_q(1, 1, 0, 512)
-        out_s(0, 1)
-        grad0(0)
-        err(3, 1, 3)
-        err_q(2, 1, 0, 512)
-        grad1(3)
-        err(3, 1, 1)
+        err(1, 1, 3)
+        err_il_s(1, 1, 256, 512)
+        err_q(0, 1, 0, 512)
         out_s(0, 0)
+        err(3, 1, 3)
+        echo_mm(3, 1, 2)
+        err_q(2, 1, 0, 512)
+        mic_scale(3, 1, 1)
+        err_il(1, 1, 0, 256)
+        mic_scale(3, 1, 2)
+        out_s(0, 1)
+        err(3, 1, 0)
+        grad0(3)
+        out_s(0, 3)
+        err_q(1, 1, 0, 512)
         grad1(0)
-        err_il(3, 1, 0, 416)
-        err_il_s(3, 1, 416, 512)
         grad1(2)
-        err_q(3, 1, 0, 512)
-        grad2(3)
-        grad2(2)
-        out_v_(1, 3)
-        grad2(0)
-        out_s(1, 2)
         grad1(1)
+        err(3, 1, 1)
+        err(3, 1, 2)
+        err_il(3, 1, 0, 352)
+        err_il_s(3, 1, 352, 512)
+        err_q(3, 1, 0, 512)
+        grad2(0)
         out_s(1, 0)
         grad2(1)
+        grad2(2)
         out_v_(1, 1)
+        out_s(1, 2)
+        grad1(3)
+        grad2(3)
+        out_v_(1, 3)

@@ -335,264 +335,264 @@ def tile_echo_nlms_gradient_s11_kernel(
             nc.sync.dma_start(out=out_v[m][:, h * W : (h + 1) * W], in_=res[:])
 
         ctx.enter_context(tc.manual_schedule())
-        load_path(0, 0)
         load_path(1, 1)
+        load_path(0, 0)
         load_path(0, 1)
         load_path(1, 0)
         load_far(0, 0, 2)
         load_far(0, 2, 4)
         load_far(1, 2, 4)
         load_far(1, 0, 2)
-        load_far(2, 2, 4)
-        load_far(2, 0, 2)
-        load_mic(1, 0)
         load_far(3, 0, 2)
-        load_mic(3, 1)
-        load_mic(2, 0)
-        load_basis()
         load_mic(0, 0)
-        load_scales()
+        load_far(2, 2, 4)
+        load_mic(1, 0)
+        load_basis()
         load_far(3, 2, 4)
+        load_far(2, 0, 2)
         load_mic(1, 1)
-        load_mic(3, 0)
-        load_mic(2, 1)
         load_mic(0, 1)
-        widen(0, 0, 0)
-        widen_v(0, 1, 0)
-        widen_v(0, 0, 1)
-        widen(0, 1, 1)
-        widen(1, 1, 3)
+        load_mic(3, 0)
+        load_mic(3, 1)
+        load_mic(2, 1)
+        load_scales()
+        load_mic(2, 0)
+        widen_v(1, 0, 3)
+        prep_steps()
+        far_turn(0, 0, 1)
         widen_v(1, 0, 2)
-        widen_v(0, 1, 3)
+        widen_v(1, 1, 3)
+        widen(1, 1, 2)
+        far_turn(0, 0, 0)
+        widen_v(0, 0, 0)
+        far_turn(0, 1, 1)
+        widen(0, 0, 1)
+        widen_v(0, 1, 0)
+        widen(0, 0, 2)
+        far_turn(0, 1, 0)
         widen_v(0, 0, 3)
         widen_v(0, 1, 2)
-        widen(1, 0, 3)
         widen_v(1, 0, 0)
-        widen_v(1, 0, 1)
-        prep_gains()
-        widen(1, 1, 1)
-        widen(1, 1, 2)
-        widen(1, 1, 0)
-        widen_v(0, 0, 2)
-        far_turn(0, 0, 0)
-        far_turn(0, 0, 1)
-        far_turn(0, 1, 1)
-        path_il(1, 0)
-        far_copy(0, 0, 0)
-        far_turn(0, 1, 0)
         path_il(0, 0)
-        far_turn(1, 1, 0)
-        path_q(1, 0)
+        widen(1, 0, 1)
+        widen(1, 1, 0)
+        path_il(1, 0)
+        widen(1, 1, 1)
         far_copy(0, 0, 1)
-        far_copy(0, 1, 1)
-        far_q(0, 1)
-        far_copy(0, 1, 0)
-        far_q(0, 0)
         path_q(0, 0)
-        far_copy(1, 1, 0)
+        far_copy(0, 0, 0)
+        far_turn(1, 1, 0)
         far_turn(1, 1, 1)
-        far_copy(1, 1, 1)
-        far_turn(1, 0, 0)
-        far_copy(1, 0, 0)
+        far_copy(0, 1, 1)
         far_turn(1, 0, 1)
-        far_turn(2, 1, 0)
-        path_il(1, 1)
-        prep_steps()
-        far_copy(1, 0, 1)
-        far_q2(1)
-        far_turn(2, 1, 1)
-        far_turn(2, 0, 0)
-        far_copy(2, 1, 0)
-        far_turn(2, 0, 1)
-        path_q(1, 1)
-        far_copy(2, 1, 1)
-        far_copy(2, 0, 0)
-        path_il(0, 1)
-        echo_mm(1, 0, 1)
-        far_copy(2, 0, 1)
-        far_q2(2)
-        mic_scale(1, 0, 2)
-        echo_mm(1, 0, 2)
-        mic_scale(1, 0, 0)
-        err(1, 0, 2)
-        mic_scale(1, 0, 1)
-        mic_scale(1, 0, 3)
-        far_turn(3, 0, 1)
-        far_copy(3, 0, 1)
-        far_turn(3, 0, 0)
-        mic_scale(2, 0, 3)
-        echo_mm(1, 0, 0)
-        comp_mm(0, 0)
-        err(1, 0, 1)
-        err(1, 0, 0)
-        mic_scale(2, 0, 1)
-        mic_scale_v(0, 0, 2)
-        comp_copy(0, 0)
-        path_q(0, 1)
-        comp_mm(0, 1)
-        mic_scale_v(0, 0, 3)
-        echo_mm(1, 0, 3)
-        err(1, 0, 3)
-        mic_scale(2, 0, 0)
-        echo_mm(0, 0, 3)
-        comp_copy(0, 1)
-        err(0, 0, 3)
-        echo_mm(0, 0, 2)
-        err(0, 0, 2)
-        far_turn(3, 1, 1)
-        far_turn(3, 1, 0)
-        err_il(1, 0, 0, 320)
-        far_copy(3, 0, 0)
-        mic_scale(0, 0, 1)
-        far_copy(3, 1, 1)
-        comp_mm(2, 0)
-        comp_mm(0, 2)
-        mic_scale_v(3, 0, 3)
-        echo_mm(0, 0, 1)
-        far_copy(3, 1, 0)
-        far_q2(3)
+        far_copy(0, 1, 0)
+        path_q(1, 0)
+        far_copy(1, 1, 0)
+        far_q(0, 1)
+        far_turn(1, 0, 0)
+        far_copy(1, 1, 1)
+        far_q(0, 0)
         echo_mm(0, 0, 0)
+        echo_mm(0, 0, 2)
+        far_copy(1, 0, 1)
+        far_copy(1, 0, 0)
         mic_scale(0, 0, 0)
-        comp_copy(0, 2)
-        comp_copy(2, 0)
-        echo_mm(2, 0, 0)
-        comp_mm(0, 3)
-        err(0, 0, 1)
-        err_il_s(1, 0, 320, 512)
-        mic_scale(3, 0, 1)
-        echo_mm(2, 0, 3)
+        widen(0, 1, 3)
+        far_turn(3, 0, 1)
+        path_il(1, 1)
+        far_q2(1)
+        widen(0, 1, 1)
+        path_q(1, 1)
+        far_turn(3, 0, 0)
+        far_turn(2, 1, 1)
         err(0, 0, 0)
-        err(2, 0, 0)
-        comp_copy(0, 3)
-        err_il_s(0, 0, 352, 512)
-        echo_mm(2, 0, 1)
-        err_q(1, 0, 0, 512)
-        mic_scale(2, 0, 2)
-        comp_mm(2, 1)
-        echo_mm(2, 0, 2)
-        comp_copy(2, 1)
-        err(2, 0, 3)
-        comp_mm(1, 0)
-        echo_mm(3, 0, 2)
-        comp_q(0)
-        mic_scale(3, 0, 2)
-        err(2, 0, 1)
-        comp_copy(1, 0)
-        mic_scale(0, 1, 3)
-        comp_mm(1, 1)
-        comp_copy(1, 1)
-        err(2, 0, 2)
-        err_il(0, 0, 0, 352)
-        echo_mm(0, 1, 3)
-        comp_mm(2, 2)
-        echo_mm(3, 0, 0)
-        err_il(2, 0, 0, 416)
-        mic_scale(0, 1, 0)
-        err(3, 0, 2)
-        comp_mm(2, 3)
-        err(0, 1, 3)
-        comp_copy(2, 2)
-        mic_scale_v(3, 0, 0)
-        echo_mm(3, 0, 1)
-        comp_mm(3, 0)
-        mic_scale(0, 1, 1)
-        err_q(0, 0, 0, 512)
-        err(3, 0, 0)
-        echo_mm(0, 1, 1)
-        comp_copy(2, 3)
-        comp_q(2)
-        err_il_s(2, 0, 416, 512)
-        mic_scale(1, 1, 2)
-        comp_mm(1, 2)
-        mic_scale(0, 1, 2)
-        err(3, 0, 1)
-        err_q(2, 0, 0, 512)
-        echo_mm(3, 0, 3)
-        comp_copy(3, 0)
+        echo_mm(1, 0, 1)
+        mic_scale(0, 0, 2)
+        err(0, 0, 2)
+        mic_scale_g(1, 0, 1)
+        mic_scale_g(0, 0, 1)
+        err(1, 0, 1)
+        far_copy(3, 0, 1)
+        echo_mm(0, 0, 1)
+        err(0, 0, 1)
+        mic_scale_g(0, 0, 3)
+        echo_mm(0, 0, 3)
+        err(0, 0, 3)
+        prep_gains()
+        echo_mm(1, 0, 0)
+        far_copy(3, 0, 0)
+        path_il_s(0, 1)
+        far_turn(3, 1, 1)
+        err_il(0, 0, 0, 256)
+        far_copy(2, 1, 1)
+        far_turn(3, 1, 0)
+        mic_scale_g(1, 0, 2)
+        mic_scale_g(1, 0, 0)
+        mic_scale_g(1, 1, 2)
+        echo_mm(1, 0, 2)
+        err(1, 0, 0)
+        echo_mm(1, 0, 3)
+        far_turn(2, 1, 0)
+        far_copy(3, 1, 1)
+        far_copy(3, 1, 0)
+        mic_scale_g(1, 0, 3)
+        path_q(0, 1)
+        far_turn(2, 0, 1)
+        err(1, 0, 2)
+        far_q2(3)
+        mic_scale_g(3, 0, 0)
+        err_il_s(0, 0, 256, 512)
+        far_turn(2, 0, 0)
         echo_mm(1, 1, 2)
-        comp_mm(3, 1)
-        err(0, 1, 1)
-        comp_copy(1, 2)
-        mic_scale(1, 1, 1)
-        err(3, 0, 3)
+        mic_scale(3, 0, 1)
+        err(1, 0, 3)
+        far_copy(2, 0, 0)
+        far_copy(2, 0, 1)
+        far_copy(2, 1, 0)
+        err_q(0, 0, 0, 512)
+        comp_mm(0, 0)
+        comp_copy(0, 0)
+        echo_mm(1, 1, 1)
         err(1, 1, 2)
-        comp_mm(1, 3)
-        mic_scale(1, 1, 0)
-        comp_copy(3, 1)
-        echo_mm(0, 1, 0)
-        err_il(3, 0, 0, 320)
-        echo_mm(0, 1, 2)
-        err(0, 1, 0)
+        mic_scale(3, 0, 3)
+        err_il(1, 0, 0, 256)
+        mic_scale_g(1, 1, 1)
+        mic_scale_g(3, 0, 2)
+        mic_scale_g(1, 1, 3)
+        echo_mm(3, 0, 0)
+        err(1, 1, 1)
+        comp_mm(1, 0)
+        comp_copy(1, 0)
         echo_mm(1, 1, 0)
-        comp_copy(1, 3)
-        comp_mm(3, 2)
-        err(0, 1, 2)
-        comp_q(1)
-        comp_mm(3, 3)
-        mic_scale(2, 1, 2)
-        err_il_s(3, 0, 320, 512)
-        echo_mm(2, 1, 0)
-        mic_scale(2, 1, 0)
-        echo_mm(2, 1, 2)
+        comp_mm(1, 1)
+        err(3, 0, 0)
+        mic_scale(1, 1, 0)
+        echo_mm(3, 0, 3)
+        comp_copy(1, 1)
+        err_il_s(1, 0, 256, 512)
+        echo_mm(1, 1, 3)
+        mic_scale_g(2, 0, 2)
+        far_q2(2)
+        comp_mm(0, 1)
+        comp_copy(0, 1)
+        mic_scale_g(2, 0, 0)
         err(1, 1, 0)
-        echo_mm(2, 1, 1)
-        comp_copy(3, 2)
-        err_q(3, 0, 0, 512)
-        err(2, 1, 0)
+        comp_mm(0, 2)
+        comp_copy(0, 2)
+        mic_scale_g(0, 1, 1)
+        echo_mm(2, 0, 2)
+        err(3, 0, 3)
+        err(1, 1, 3)
+        err_q(1, 0, 0, 512)
+        echo_mm(3, 0, 2)
+        mic_scale(2, 0, 1)
+        mic_scale(0, 1, 3)
+        comp_mm(0, 3)
+        comp_copy(0, 3)
+        mic_scale_g(2, 0, 3)
+        echo_mm(3, 0, 1)
+        err(2, 0, 2)
+        comp_mm(1, 2)
+        comp_copy(1, 2)
+        echo_mm(2, 0, 1)
+        err_il_s(1, 1, 256, 512)
+        err_il(1, 1, 0, 256)
+        echo_mm(2, 0, 0)
+        comp_mm(2, 0)
+        err(3, 0, 2)
+        err(3, 0, 1)
+        mic_scale_g(3, 1, 2)
+        comp_mm(1, 3)
+        comp_q(0)
+        err(2, 0, 1)
+        comp_copy(2, 0)
+        echo_mm(2, 0, 3)
+        echo_mm(0, 1, 1)
+        mic_scale_g(0, 1, 2)
+        comp_copy(1, 3)
+        comp_mm(2, 1)
+        err_il(3, 0, 0, 256)
+        err(2, 0, 0)
+        err_il_s(3, 0, 256, 512)
+        echo_mm(0, 1, 2)
+        mic_scale_g(2, 1, 2)
+        err(2, 0, 3)
+        comp_copy(2, 1)
+        comp_mm(3, 0)
+        err_q(1, 1, 0, 512)
+        mic_scale_g(2, 1, 0)
+        err_il_s(2, 0, 256, 512)
+        echo_mm(3, 1, 2)
+        comp_copy(3, 0)
+        echo_mm(0, 1, 3)
+        err(0, 1, 1)
+        comp_q(1)
+        comp_mm(3, 1)
+        err(0, 1, 2)
+        err_il(2, 0, 0, 256)
+        mic_scale_g(3, 1, 0)
+        echo_mm(0, 1, 0)
+        mic_scale(0, 1, 0)
+        comp_copy(3, 1)
         mic_scale(2, 1, 1)
+        comp_mm(3, 2)
+        comp_copy(3, 2)
+        err(3, 1, 2)
+        echo_mm(2, 1, 0)
+        err(0, 1, 3)
+        err(0, 1, 0)
+        comp_mm(3, 3)
         comp_copy(3, 3)
         echo_mm(2, 1, 3)
-        err(2, 1, 2)
-        echo_mm(1, 1, 3)
+        comp_mm(2, 2)
+        err_q(2, 0, 0, 512)
+        err(2, 1, 0)
         mic_scale(2, 1, 3)
-        err(2, 1, 1)
-        echo_mm(1, 1, 1)
-        err_il_s(0, 1, 256, 512)
-        mic_scale(1, 1, 3)
+        echo_mm(2, 1, 2)
+        comp_mm(2, 3)
+        comp_copy(2, 2)
+        err_q(3, 0, 0, 512)
         comp_q(3)
-        grad0(2)
+        echo_mm(2, 1, 1)
         err(2, 1, 3)
-        err_il_s(2, 1, 256, 512)
-        err_il(0, 1, 0, 256)
-        err_il(2, 1, 0, 256)
-        echo_mm(3, 1, 3)
-        mic_scale(3, 1, 3)
-        grad0(0)
-        err(1, 1, 1)
-        mic_scale(3, 1, 0)
+        comp_copy(2, 3)
+        err(2, 1, 2)
+        err_il_s(0, 1, 384, 512)
         echo_mm(3, 1, 0)
         echo_mm(3, 1, 1)
-        grad0(1)
-        out_s(0, 2)
-        err(1, 1, 3)
-        err_il_s(1, 1, 256, 512)
-        err_q(0, 1, 0, 512)
-        out_s(0, 0)
-        err(3, 1, 3)
-        echo_mm(3, 1, 2)
-        err_q(2, 1, 0, 512)
+        err(2, 1, 1)
+        echo_mm(3, 1, 3)
+        comp_q(2)
+        grad0(2)
+        err_il_s(2, 1, 256, 512)
         mic_scale(3, 1, 1)
-        err_il(1, 1, 0, 256)
-        mic_scale(3, 1, 2)
-        out_s(0, 1)
+        err_il(0, 1, 0, 384)
         err(3, 1, 0)
-        grad0(3)
-        out_s(0, 3)
-        err_q(1, 1, 0, 512)
-        grad1(0)
-        grad1(2)
-        grad1(1)
+        err_il(2, 1, 0, 256)
+        err_q(0, 1, 0, 512)
+        out_s(0, 2)
         err(3, 1, 1)
-        err(3, 1, 2)
-        err_il(3, 1, 0, 352)
+        grad0(0)
+        out_s(0, 0)
+        grad0(1)
+        grad0(3)
+        err_q(2, 1, 0, 512)
+        grad1(1)
+        grad1(3)
+        out_s(0, 1)
+        grad1(0)
+        mic_scale_g(3, 1, 3)
+        err(3, 1, 3)
         err_il_s(3, 1, 352, 512)
+        err_il(3, 1, 0, 352)
         err_q(3, 1, 0, 512)
+        out_s(0, 3)
         grad2(0)
         out_s(1, 0)
         grad2(1)
-        grad2(2)
         out_v_(1, 1)
-        out_s(1, 2)
-        grad1(3)
         grad2(3)
         out_v_(1, 3)
+        grad1(2)
+        grad2(2)
+        out_s(1, 2)

from contextlib import ExitStack

import concourse.mybir as mybir
from concourse.masks import make_identity

T, K, R, C = 2048, 1024, 512, 1024
FLOPS = 2 * T * K * C + 2 * T * K * R + 2 * T * R * C

F32 = mybir.dt.float32
BF16 = mybir.dt.bfloat16
I32 = mybir.dt.int32
U32 = mybir.dt.uint32
U8 = mybir.dt.uint8
FP8 = mybir.dt.float8_e4m3fn
FP8X4 = mybir.dt.float8_e4m3fn_x4
FP4X4 = mybir.dt.float4_e2m1fn_x4
ALU = mybir.AluOpType
COPY = mybir.ActivationFunctionType.Copy

P = 128
PACK = 4
PASS = P * PACK
NG = T // PASS
NK = K // PASS
NH = 2
W = C // NH


def tile_echo_nlms_gradient_s11_kernel(
    tc, far, mic, path_bytes, path_scale, basis_words, basis_scales, step, gain, out
):
    nc = tc.nc
    with ExitStack() as ctx:
        keep = ctx.enter_context(tc.tile_pool(name="keep", bufs=1))
        work = ctx.enter_context(tc.tile_pool(name="work", bufs=2))
        turn = ctx.enter_context(tc.psum_pool(name="turn", bufs=3))
        comp = ctx.enter_context(tc.psum_pool(name="comp", bufs=2))
        echo = ctx.enter_context(tc.psum_pool(name="echo", bufs=3))

        ident = keep.tile([P, P], F32, name="ident")
        make_identity(nc, ident[:])
        pscale = keep.tile([P, NK, PACK], F32, name="pscale")
        nc.scalar.dma_start(out=pscale[:], in_=path_scale.rearrange("(g p t) o -> p g (t o)", p=P, t=PACK))
        step_bf = keep.tile([P, NG, PACK], BF16, name="step_bf")
        nc.scalar.dma_start(out=step_bf[:], in_=step.rearrange("(g p j) -> p g j", p=P, j=PACK))
        gain_bf = keep.tile([P, PACK], BF16, name="gain_bf")
        nc.scalar.dma_start(out=gain_bf[:], in_=gain.rearrange("(q m) -> q m", m=PACK))
        bscale = keep.tile([P, NK, R], U8, name="bscale", align_bytes=64)
        nc.vector.memset(bscale[:].rearrange("p g n -> p (g n)").bitcast(I32), 0)

        far_t = [keep.tile([P, PACK, K], BF16, name=f"far{g}") for g in range(NG)]
        mic_t = [[keep.tile([P, PACK, W], BF16, name=f"mic{g}_{h}") for h in range(NH)] for g in range(NG)]
        pbytes = [keep.tile([P, PACK, C], U8, name=f"pbytes{g}", align_bytes=64) for g in range(NK)]
        bwords = keep.tile([P, NK, 2 * R], U8, name="bwords", align_bytes=64)
        far_v = far.rearrange("(g p j) k -> g p j k", p=P, j=PACK)
        mic_v = mic.rearrange("(g p j) c -> g p j c", p=P, j=PACK)
        path_v = path_bytes.rearrange("(g p t) c -> g p t c", p=P, t=PACK)

        def load_far(g, lo, hi):
            nc.sync.dma_start(out=far_t[g][:, lo:hi, :], in_=far_v[g][:, lo:hi, :])

        def load_mic(g, h):
            nc.sync.dma_start(out=mic_t[g][h][:], in_=mic_v[g][:, :, h * W : (h + 1) * W])

        def load_path(g, half):
            ts = slice(2 * half, 2 * half + 2)
            nc.sync.dma_start(out=pbytes[g][:, ts, :], in_=path_v[g][:, ts, :])

        def load_basis():
            nc.sync.dma_start(out=bwords[:], in_=basis_words.rearrange("g p n -> p g n"))

        def load_scales():
            for q in range(4):
                nc.sync.dma_start(
                    out=bscale[32 * q : 32 * q + 4, :, :].bitcast(I32),
                    in_=basis_scales[:, 4 * q : 4 * q + 4, :].bitcast(I32).rearrange("g q n -> q g n"),
                )


        steps = keep.tile([P, NG, PACK], F32, name="steps")
        negstep = keep.tile([P, NG, PACK], F32, name="negstep")
        gains = keep.tile([P, PACK], F32, name="gains")

        def prep_steps():
            nc.gpsimd.tensor_copy(out=steps[:], in_=step_bf[:])
            nc.gpsimd.tensor_scalar(out=negstep[:], in0=step_bf[:], scalar1=-1.0, scalar2=0.0, op0=ALU.mult, op1=ALU.add)

        def prep_gains():
            nc.gpsimd.tensor_copy(out=gains[:], in_=gain_bf[:])


        x_codes = [keep.tile([P, NK, PASS], U32, name=f"x_codes{g}", align_bytes=64) for g in range(NG)]
        x_scales = [keep.tile([P, NK, PASS], U8, name=f"x_scales{g}", align_bytes=64) for g in range(NG)]
        p_codes = [[keep.tile([P, W], U32, name=f"p_codes{g}_{h}", align_bytes=64) for h in range(NH)] for g in range(NK)]
        p_scales = [[keep.tile([P, W], U8, name=f"p_scales{g}_{h}", align_bytes=64) for h in range(NH)] for g in range(NK)]
        u_codes = [keep.tile([P, R], U32, name=f"u_codes{g}", align_bytes=64) for g in range(NG)]
        u_scales = [keep.tile([P, R], U8, name=f"u_scales{g}", align_bytes=64) for g in range(NG)]
        e_codes = [[keep.tile([P, W], U32, name=f"e_codes{g}_{h}", align_bytes=64) for h in range(NH)] for g in range(NG)]
        e_scales = [[keep.tile([P, W], U8, name=f"e_scales{g}_{h}", align_bytes=64) for h in range(NH)] for g in range(NG)]

        pwide = [[keep.tile([P, PACK, W], BF16, name=f"pwide{g}_{h}") for h in range(NH)] for g in range(NK)]
        pil = {}

        def widen_v(g, h, t):
            nc.vector.tensor_scalar(
                out=pwide[g][h][:, t, :],
                in0=pbytes[g][:, t, h * W : (h + 1) * W].bitcast(FP8),
                scalar1=pscale[:, g, t : t + 1],
                scalar2=None,
                op0=ALU.mult,
            )

        def widen(g, h, t):
            nc.scalar.activation(
                out=pwide[g][h][:, t, :],
                in_=pbytes[g][:, t, h * W : (h + 1) * W].bitcast(FP8),
                func=COPY,
                scale=pscale[:, g, t : t + 1],
            )

        def path_il(g, h):
            pil[g, h] = work.tile([P, W, PACK], BF16, name="p_grouped", align_bytes=64)
            nc.vector.tensor_copy(
                out=pil[g, h][:].rearrange("p (c i) t -> p c t i", i=4),
                in_=pwide[g][h][:].rearrange("p t (c i) -> p c t i", i=4),
            )

        def path_il_s(g, h):
            pil[g, h] = work.tile([P, W, PACK], BF16, name="p_grouped", align_bytes=64)
            nc.scalar.copy(
                out=pil[g, h][:].rearrange("p (c i) t -> p c t i", i=4),
                in_=pwide[g][h][:].rearrange("p t (c i) -> p c t i", i=4),
            )

        def path_q(g, h):
            nc.vector.quantize_mx(
                out=p_codes[g][h][:].bitcast(FP8X4),
                scales=p_scales[g][h][:],
                in_=pil[g, h][:].rearrange("p c t -> p (c t)"),
            )

        xg = {}

        xbank = {}

        def far_turn(g, half, k):
            words = far_t[g][:].bitcast(F32)
            bank = turn.tile([P, 2, 2, P], F32, name="turn_bank")
            for jj in range(2):
                for u in range(2):
                    nc.tensor.transpose(
                        bank[:, jj, u, :], words[:, 2 * half + jj, 256 * k + u : 256 * (k + 1) : 2], ident[:]
                    )
            xbank[g, half, k] = bank

        def far_copy(g, half, k):
            if g not in xg:
                xg[g] = work.tile([P, NK, PACK, P, 2], F32, name="x_grouped", align_bytes=64)
            nc.scalar.copy(
                out=xg[g][:, k, 2 * half : 2 * half + 2, :, :],
                in_=xbank[g, half, k][:].rearrange("p j u n -> p j n u"),
            )

        def far_q(g, k):
            flat = xg[g][:].rearrange("p k j n u -> p k (j n u)").bitcast(BF16)
            nc.vector.quantize_mx(
                out=x_codes[g][:, k, :].bitcast(FP8X4), scales=x_scales[g][:, k, :], in_=flat[:, k, :]
            )

        def far_q2(g):
            nc.vector.quantize_mx(
                out=x_codes[g][:].rearrange("p k n -> p (k n)").bitcast(FP8X4),
                scales=x_scales[g][:].rearrange("p k n -> p (k n)"),
                in_=xg[g][:].rearrange("p k j n u -> p (k j n u)").bitcast(BF16),
            )

        ug = {}

        ubank = {}

        def comp_mm(g, chunk):
            bank = comp.tile([P, PACK, P], F32, name="comp_bank")
            cols = slice(chunk * P, (chunk + 1) * P)
            for j in range(PACK):
                for k in range(NK):
                    nc.tensor.matmul_mx(
                        out=bank[:, j, :],
                        lhsT=x_codes[g][:, k, j * P : (j + 1) * P].bitcast(FP8X4),
                        lhsT_scale=x_scales[g][:, k, j * P : (j + 1) * P],
                        rhs=bwords[:, k, 2 * chunk * P : 2 * (chunk + 1) * P].bitcast(FP4X4),
                        rhs_scale=bscale[:, k, cols],
                        start=(k == 0),
                        stop=(k == NK - 1),
                    )
            ubank[g, chunk] = bank

        def comp_copy(g, chunk):
            if g not in ug:
                ug[g] = work.tile([P, 4, P, PACK], BF16, name="u_grouped", align_bytes=64)
            nc.scalar.copy(
                out=ug[g][:, :, 32 * chunk : 32 * (chunk + 1), :],
                in_=ubank[g, chunk][:].rearrange("p j (q m) -> p m q j", m=4),
            )

        def comp_q(g):
            nc.vector.quantize_mx(
                out=u_codes[g][:].bitcast(FP8X4),
                scales=u_scales[g][:],
                in_=ug[g][:].rearrange("p m q j -> p (m q j)"),
            )

        ms = {}
        ep = {}
        eg = {}
        ebank = {}

        def mic_scale_v(g, h, j):
            if (g, h) not in ms:
                ms[g, h] = work.tile([P, PACK, W], F32, name="mic_scaled", bufs=3)
            nc.vector.tensor_scalar(
                out=ms[g, h][:, j, :], in0=mic_t[g][h][:, j, :], scalar1=steps[:, g, j : j + 1], scalar2=None, op0=ALU.mult
            )

        def mic_scale_g(g, h, j):
            if (g, h) not in ms:
                ms[g, h] = work.tile([P, PACK, W], F32, name="mic_scaled", bufs=3)
            nc.gpsimd.tensor_scalar(
                out=ms[g, h][:, j, :],
                in0=mic_t[g][h][:, j, :],
                scalar1=steps[:, g, j : j + 1],
                scalar2=0.0,
                op0=ALU.mult,
                op1=ALU.add,
            )

        def mic_scale(g, h, j):
            if (g, h) not in ms:
                ms[g, h] = work.tile([P, PACK, W], F32, name="mic_scaled", bufs=3)
            nc.scalar.activation(
                out=ms[g, h][:, j, :], in_=mic_t[g][h][:, j, :], func=COPY, scale=steps[:, g, j : j + 1]
            )

        def echo_mm(g, h, j):
            bank = echo.tile([P, W], F32, name="echo_bank")
            for k in range(NK):
                nc.tensor.matmul_mx(
                    out=bank[:],
                    lhsT=x_codes[g][:, k, j * P : (j + 1) * P].bitcast(FP8X4),
                    lhsT_scale=x_scales[g][:, k, j * P : (j + 1) * P],
                    rhs=p_codes[k][h][:].bitcast(FP8X4),
                    rhs_scale=p_scales[k][h][:],
                    start=(k == 0),
                    stop=(k == NK - 1),
                )
            ebank[g, h, j] = bank

        def err(g, h, j):
            if (g, h) not in ep:
                ep[g, h] = work.tile([P, PACK, W], BF16, name="e_rows", bufs=3)
            nc.vector.scalar_tensor_tensor(
                out=ep[g, h][:, j, :],
                in0=ebank[g, h, j][:],
                scalar=negstep[:, g, j : j + 1],
                in1=ms[g, h][:, j, :],
                op0=ALU.mult,
                op1=ALU.add,
            )

        def err_il(g, h, lo, hi):
            if (g, h) not in eg:
                eg[g, h] = work.tile([P, W, PACK], BF16, name="e_grouped", align_bytes=64)
            nc.vector.tensor_copy(
                out=eg[g, h][:, lo:hi, :].rearrange("p (c i) j -> p c j i", i=4),
                in_=ep[g, h][:, :, lo:hi].rearrange("p j (c i) -> p c j i", i=4),
            )

        def err_il_s(g, h, lo, hi):
            if (g, h) not in eg:
                eg[g, h] = work.tile([P, W, PACK], BF16, name="e_grouped", align_bytes=64)
            nc.scalar.copy(
                out=eg[g, h][:, lo:hi, :].rearrange("p (c i) j -> p c j i", i=4),
                in_=ep[g, h][:, :, lo:hi].rearrange("p j (c i) -> p c j i", i=4),
            )

        def err_q(g, h, lo=0, hi=W):
            nc.vector.quantize_mx(
                out=e_codes[g][h][:, lo:hi].bitcast(FP8X4),
                scales=e_scales[g][h][:, lo:hi],
                in_=eg[g, h][:, lo:hi, :].rearrange("p c j -> p (c j)"),
            )

        out_v = out.rearrange("(q m) c -> m q c", m=4)

        def grad_mm(bank, g, h, m):
            nc.tensor.matmul_mx(
                out=bank[:],
                lhsT=u_codes[g][:, m * P : (m + 1) * P].bitcast(FP8X4),
                lhsT_scale=u_scales[g][:, m * P : (m + 1) * P],
                rhs=e_codes[g][h][:].bitcast(FP8X4),
                rhs_scale=e_scales[g][h][:],
                start=(g == 0),
                stop=(g == NG - 1),
            )

        gbank = {}

        def grad0(m):
            bank = comp.tile([P, W], F32, name="comp_bank")
            for g in range(NG):
                grad_mm(bank, g, 0, m)
            gbank[0, m] = bank

        def grad1(m):
            if m < 2:
                bank = turn.tile([P, W], F32, name="turn_bank")
            else:
                bank = comp.tile([P, W], F32, name="comp_bank")
            for g in range(NG - 1):
                grad_mm(bank, g, 1, m)
            gbank[1, m] = bank

        def grad2(m):
            grad_mm(gbank[1, m], NG - 1, 1, m)

        def out_s(h, m):
            res = work.tile([P, W], F32, name="res", bufs=4)
            nc.scalar.activation(out=res[:], in_=gbank[h, m][:], func=COPY, scale=gains[:, m : m + 1])
            nc.sync.dma_start(out=out_v[m][:, h * W : (h + 1) * W], in_=res[:])

        def out_v_(h, m):
            res = work.tile([P, W], F32, name="res", bufs=4)
            nc.vector.tensor_scalar(
                out=res[:], in0=gbank[h, m][:], scalar1=gains[:, m : m + 1], scalar2=None, op0=ALU.mult
            )
            nc.sync.dma_start(out=out_v[m][:, h * W : (h + 1) * W], in_=res[:])

        ctx.enter_context(tc.manual_schedule())
        load_path(1, 1)
        load_path(0, 0)
        load_path(0, 1)
        load_path(1, 0)
        load_far(0, 0, 2)
        load_far(0, 2, 4)
        load_far(1, 2, 4)
        load_far(1, 0, 2)
        load_far(3, 0, 2)
        load_mic(0, 0)
        load_far(2, 2, 4)
        load_mic(1, 0)
        load_basis()
        load_far(3, 2, 4)
        load_far(2, 0, 2)
        load_mic(1, 1)
        load_mic(0, 1)
        load_mic(3, 0)
        load_mic(3, 1)
        load_mic(2, 1)
        load_scales()
        load_mic(2, 0)
        widen_v(1, 0, 3)
        prep_steps()
        far_turn(0, 0, 1)
        widen_v(1, 0, 2)
        widen_v(1, 1, 3)
        widen(1, 1, 2)
        far_turn(0, 0, 0)
        widen_v(0, 0, 0)
        far_turn(0, 1, 1)
        widen(0, 0, 1)
        widen_v(0, 1, 0)
        widen(0, 0, 2)
        far_turn(0, 1, 0)
        widen_v(0, 0, 3)
        widen_v(0, 1, 2)
        widen_v(1, 0, 0)
        path_il(0, 0)
        widen(1, 0, 1)
        widen(1, 1, 0)
        path_il(1, 0)
        widen(1, 1, 1)
        far_copy(0, 0, 1)
        path_q(0, 0)
        far_copy(0, 0, 0)
        far_turn(1, 1, 0)
        far_turn(1, 1, 1)
        far_copy(0, 1, 1)
        far_turn(1, 0, 1)
        far_copy(0, 1, 0)
        path_q(1, 0)
        far_copy(1, 1, 0)
        far_q(0, 1)
        far_turn(1, 0, 0)
        far_copy(1, 1, 1)
        far_q(0, 0)
        echo_mm(0, 0, 0)
        echo_mm(0, 0, 2)
        far_copy(1, 0, 1)
        far_copy(1, 0, 0)
        mic_scale(0, 0, 0)
        widen(0, 1, 3)
        far_turn(3, 0, 1)
        path_il(1, 1)
        far_q2(1)
        widen(0, 1, 1)
        path_q(1, 1)
        far_turn(3, 0, 0)
        far_turn(2, 1, 1)
        err(0, 0, 0)
        echo_mm(1, 0, 1)
        mic_scale(0, 0, 2)
        err(0, 0, 2)
        mic_scale_g(1, 0, 1)
        mic_scale_g(0, 0, 1)
        err(1, 0, 1)
        far_copy(3, 0, 1)
        echo_mm(0, 0, 1)
        err(0, 0, 1)
        mic_scale_g(0, 0, 3)
        echo_mm(0, 0, 3)
        err(0, 0, 3)
        prep_gains()
        echo_mm(1, 0, 0)
        far_copy(3, 0, 0)
        path_il_s(0, 1)
        far_turn(3, 1, 1)
        err_il(0, 0, 0, 256)
        far_copy(2, 1, 1)
        far_turn(3, 1, 0)
        mic_scale_g(1, 0, 2)
        mic_scale_g(1, 0, 0)
        mic_scale_g(1, 1, 2)
        echo_mm(1, 0, 2)
        err(1, 0, 0)
        echo_mm(1, 0, 3)
        far_turn(2, 1, 0)
        far_copy(3, 1, 1)
        far_copy(3, 1, 0)
        mic_scale_g(1, 0, 3)
        path_q(0, 1)
        far_turn(2, 0, 1)
        err(1, 0, 2)
        far_q2(3)
        mic_scale_g(3, 0, 0)
        err_il_s(0, 0, 256, 512)
        far_turn(2, 0, 0)
        echo_mm(1, 1, 2)
        mic_scale(3, 0, 1)
        err(1, 0, 3)
        far_copy(2, 0, 0)
        far_copy(2, 0, 1)
        far_copy(2, 1, 0)
        err_q(0, 0, 0, 512)
        comp_mm(0, 0)
        comp_copy(0, 0)
        echo_mm(1, 1, 1)
        err(1, 1, 2)
        mic_scale(3, 0, 3)
        err_il(1, 0, 0, 256)
        mic_scale_g(1, 1, 1)
        mic_scale_g(3, 0, 2)
        mic_scale_g(1, 1, 3)
        echo_mm(3, 0, 0)
        err(1, 1, 1)
        comp_mm(1, 0)
        comp_copy(1, 0)
        echo_mm(1, 1, 0)
        comp_mm(1, 1)
        err(3, 0, 0)
        mic_scale(1, 1, 0)
        echo_mm(3, 0, 3)
        comp_copy(1, 1)
        err_il_s(1, 0, 256, 512)
        echo_mm(1, 1, 3)
        mic_scale_g(2, 0, 2)
        far_q2(2)
        comp_mm(0, 1)
        comp_copy(0, 1)
        mic_scale_g(2, 0, 0)
        err(1, 1, 0)
        comp_mm(0, 2)
        comp_copy(0, 2)
        mic_scale_g(0, 1, 1)
        echo_mm(2, 0, 2)
        err(3, 0, 3)
        err(1, 1, 3)
        err_q(1, 0, 0, 512)
        echo_mm(3, 0, 2)
        mic_scale(2, 0, 1)
        mic_scale(0, 1, 3)
        comp_mm(0, 3)
        comp_copy(0, 3)
        mic_scale_g(2, 0, 3)
        echo_mm(3, 0, 1)
        err(2, 0, 2)
        comp_mm(1, 2)
        comp_copy(1, 2)
        echo_mm(2, 0, 1)
        err_il_s(1, 1, 256, 512)
        err_il(1, 1, 0, 256)
        echo_mm(2, 0, 0)
        comp_mm(2, 0)
        err(3, 0, 2)
        err(3, 0, 1)
        mic_scale_g(3, 1, 2)
        comp_mm(1, 3)
        comp_q(0)
        err(2, 0, 1)
        comp_copy(2, 0)
        echo_mm(2, 0, 3)
        echo_mm(0, 1, 1)
        mic_scale_g(0, 1, 2)
        comp_copy(1, 3)
        comp_mm(2, 1)
        err_il(3, 0, 0, 256)
        err(2, 0, 0)
        err_il_s(3, 0, 256, 512)
        echo_mm(0, 1, 2)
        mic_scale_g(2, 1, 2)
        err(2, 0, 3)
        comp_copy(2, 1)
        comp_mm(3, 0)
        err_q(1, 1, 0, 512)
        mic_scale_g(2, 1, 0)
        err_il_s(2, 0, 256, 512)
        echo_mm(3, 1, 2)
        comp_copy(3, 0)
        echo_mm(0, 1, 3)
        err(0, 1, 1)
        comp_q(1)
        comp_mm(3, 1)
        err(0, 1, 2)
        err_il(2, 0, 0, 256)
        mic_scale_g(3, 1, 0)
        echo_mm(0, 1, 0)
        mic_scale(0, 1, 0)
        comp_copy(3, 1)
        mic_scale(2, 1, 1)
        comp_mm(3, 2)
        comp_copy(3, 2)
        err(3, 1, 2)
        echo_mm(2, 1, 0)
        err(0, 1, 3)
        err(0, 1, 0)
        comp_mm(3, 3)
        comp_copy(3, 3)
        echo_mm(2, 1, 3)
        comp_mm(2, 2)
        err_q(2, 0, 0, 512)
        err(2, 1, 0)
        mic_scale(2, 1, 3)
        echo_mm(2, 1, 2)
        comp_mm(2, 3)
        comp_copy(2, 2)
        err_q(3, 0, 0, 512)
        comp_q(3)
        echo_mm(2, 1, 1)
        err(2, 1, 3)
        comp_copy(2, 3)
        err(2, 1, 2)
        err_il_s(0, 1, 384, 512)
        echo_mm(3, 1, 0)
        echo_mm(3, 1, 1)
        err(2, 1, 1)
        echo_mm(3, 1, 3)
        comp_q(2)
        grad0(2)
        err_il_s(2, 1, 256, 512)
        mic_scale(3, 1, 1)
        err_il(0, 1, 0, 384)
        err(3, 1, 0)
        err_il(2, 1, 0, 256)
        err_q(0, 1, 0, 512)
        out_s(0, 2)
        err(3, 1, 1)
        grad0(0)
        out_s(0, 0)
        grad0(1)
        grad0(3)
        err_q(2, 1, 0, 512)
        grad1(1)
        grad1(3)
        out_s(0, 1)
        grad1(0)
        mic_scale_g(3, 1, 3)
        err(3, 1, 3)
        err_il_s(3, 1, 352, 512)
        err_il(3, 1, 0, 352)
        err_q(3, 1, 0, 512)
        out_s(0, 3)
        grad2(0)
        out_s(1, 0)
        grad2(1)
        out_v_(1, 1)
        grad2(3)
        out_v_(1, 3)
        grad1(2)
        grad2(2)
        out_s(1, 2)
